import numpy as np
import ml_dtypes


def mxq(x, axis, fmt="e4m3"):
    dtype, down = {"e4m3": (ml_dtypes.float8_e4m3fn, 7), "e5m2": (ml_dtypes.float8_e5m2, 14)}[fmt]
    v = np.moveaxis(np.asarray(x, np.float32).astype(ml_dtypes.bfloat16).astype(np.float64), axis, -1)
    blocks = v.reshape(v.shape[:-1] + (-1, 32))
    amax = np.abs(blocks).max(-1, keepdims=True)
    byte = np.maximum(np.where(amax > 0, np.frexp(amax)[1] - 1 + 127, 0) - down, 1)
    scale = np.exp2(byte - 127.0)
    codes = (blocks / scale).astype(np.float32).astype(dtype).astype(np.float64)
    return np.moveaxis((codes * scale).reshape(v.shape), -1, axis)


WIDE = False


def mx_kscale(k):
    if not WIDE:
        return np.ones(k)
    levels = np.array([10, -10, 5, -5, 0])
    if k % 512:
        return np.exp2(np.random.permutation(np.resize(levels, k // 32))).repeat(32)
    a = np.empty((k // 512, 16))
    for p in range(k // 512):
        a[p, :8] = np.random.permutation(np.resize(levels, 8))
        for g in range(8):
            far = levels[np.abs(levels - a[p, g]) >= 10]
            a[p, g + 8] = far[np.random.randint(len(far))]
    return np.exp2(a.ravel()).repeat(32)


def f64(x):
    return np.asarray(x).astype(np.float64)


def striped(idx):
    return np.tile(idx.reshape(-1, 16).T, (8, 1)).astype(np.uint16)


def unstriped(offs):
    return offs[:16].T.reshape(-1).astype(np.int64)


E2M1 = np.array([0.0, 0.5, 1.0, 1.5, 2.0, 3.0, 4.0, 6.0, -0.0, -0.5, -1.0, -1.5, -2.0, -3.0, -4.0, -6.0])


def pack_weight(w, fmt):
    k, n = w.shape
    w = f64(np.asarray(w, np.float32).astype(ml_dtypes.bfloat16)).reshape(k // 32, 32, n)
    amax = np.abs(w).max(1)
    if fmt == "e4m3":
        byte = np.frexp(amax)[1] - 1 + 127 - 7
    else:
        mant, ex = np.frexp(amax / 6.0)
        byte = np.where(mant > 0.5, ex, ex - 1) + 127
    byte = np.clip(np.where(amax > 0, byte, 1), 1, 254)
    scaled = (w * np.exp2(127.0 - byte)[:, None, :]).reshape(k, n).astype(np.float32)
    by_word = np.ascontiguousarray(scaled.reshape(k // 512, 128, 4, n).transpose(0, 1, 3, 2))
    if fmt == "e4m3":
        words = by_word.astype(ml_dtypes.float8_e4m3fn).view(np.uint8)
    else:
        c = by_word.astype(ml_dtypes.float4_e2m1fn).view(np.uint8) & 0xF
        words = (c[..., 0::2] | (c[..., 1::2] << 4)).reshape(k // 512, 128, 2 * n)
    return np.ascontiguousarray(words), np.ascontiguousarray(byte.astype(np.uint8).reshape(k // 512, 16, n))


def unpack_weight(words, scales, fmt):
    g, _, n = scales.shape
    words = np.ascontiguousarray(words).reshape(g, 128, n, -1)
    if fmt == "e4m3":
        vals = words.view(ml_dtypes.float8_e4m3fn).astype(np.float64)
    else:
        nib = np.empty((g, 128, n, 4), np.uint8)
        nib[..., 0::2] = words & 0xF
        nib[..., 1::2] = words >> 4
        vals = E2M1[nib]
    vals = vals * np.repeat(np.exp2(scales.astype(np.float64) - 127.0), 8, axis=1)[..., None]
    return vals.transpose(0, 1, 3, 2).reshape(g * 512, n)


def gelu(v):
    return 0.5 * v * (1.0 + np.tanh(np.sqrt(2.0 / np.pi) * (v + 0.044715 * v**3)))


K, T, E, C, H, N = 512, 768, 6, 256, 512, 512


def by_expert(wq, xq):
    return np.concatenate([wq[e].T @ xq[:, e * C:(e + 1) * C] for e in range(E)], axis=1)


def setup_inputs():
    n = np.random.standard_normal
    s = mx_kscale(K)
    u = mx_kscale(H)
    first = np.random.permutation(np.repeat(np.arange(E), T // E))
    second = (first + 1 + np.random.permutation(np.repeat(np.arange(E - 1), -(-T // (E - 1)))[:T])) % E
    while np.bincount(second, minlength=E).max() != T // E:
        load = np.bincount(second, minlength=E); hi, lo = int(load.argmax()), int(load.argmin())
        t = np.flatnonzero((second == hi) & (first != lo))[0]; second[t] = lo
    slot_token = np.empty(E * C, np.int64); pos = np.empty((2, T), np.int64); fill = np.zeros(E, np.int64)
    place = np.stack([np.random.permutation(C) for _ in range(E)])
    for r, deal in enumerate((first, second)):
        for t in np.random.permutation(T):
            e = deal[t]; j = e * C + place[e, fill[e]]; fill[e] += 1; slot_token[j] = t; pos[r, t] = j
    g = np.random.uniform(0.2, 0.8, T)
    x = pack_weight(n((K, T)) * s[:, None], "e4m3")
    w1 = pack_weight(n((K, H)) / np.sqrt(K) / s[:, None] * u, "e4m3")
    return {
        "x_words": x[0],
        "x_scales": x[1],
        "w1_words": w1[0],
        "w1_scales": w1[1],
        "w2": (n((E, H, N)) / np.sqrt(H) / u[None, :, None]).astype(np.float32),
        "gate": np.stack([np.tile(g, (128, 1)), np.tile(1.0 - g, (128, 1))]).astype(np.float32),
        "offs": striped(slot_token),
        "pos1": striped(pos[0]),
        "pos2": striped(pos[1]),
    }


def reference(x_words, x_scales, w1_words, w1_scales, w2, gate, offs, pos1, pos2):
    w1 = unpack_weight(w1_words, w1_scales, "e4m3")
    w2q = mxq(f64(w2), 1, "e4m3")
    idx = unstriped(offs)
    x = unpack_weight(x_words, x_scales, "e4m3")
    h = gelu(w1.T @ x)
    y = by_expert(w2q, mxq(h[:, idx], 0, "e4m3"))
    out = sum(f64(gate[r, :1]) * y[:, unstriped(p)] for r, p in enumerate((pos1, pos2)))
    return out

@@ -1,0 +1,287 @@
+from contextlib import ExitStack
+
+import concourse.mybir as mybir
+from concourse.masks import make_identity
+
+K, T, E, C, H, N = 512, 768, 6, 256, 512, 512
+S = E * C
+P = 128
+PACK = 4
+FLOPS = 2 * K * H * T + 2 * H * N * S
+
+F32 = mybir.dt.float32
+BF16 = mybir.dt.bfloat16
+I32 = mybir.dt.int32
+U32 = mybir.dt.uint32
+U16 = mybir.dt.uint16
+U8 = mybir.dt.uint8
+FP8X4 = mybir.dt.float8_e4m3fn_x4
+GELU = mybir.ActivationFunctionType.Gelu_apprx_tanh
+MULT = mybir.AluOpType.mult
+ADD = mybir.AluOpType.add
+
+NB = N // P
+HALF = N // 2
+TOK = 256
+PIECE = 2 * C
+
+
+def load_scale_rows(nc, plane, rows):
+    width = rows.shape[1] // 4
+    by_row = rows.bitcast(I32).rearrange("(q r) w -> r q w", r=4)
+    for r in range(4):
+        nc.sync.dma_start(
+            out=plane[:].bitcast(I32)[r:P:4, :],
+            in_=by_row[r].unsqueeze(1).broadcast_to([4, 8, width]),
+        )
+
+
+def tile_moe_sup_lin_gelu_kernel(
+    tc, x_words, x_scales, w1_words, w1_scales, w2, gate, offs, pos1, pos2, out
+):
+    nc = tc.nc
+    with ExitStack() as ctx:
+        keep = ctx.enter_context(tc.tile_pool(name="keep", bufs=1))
+        psum = ctx.enter_context(tc.psum_pool(name="psum", bufs=1))
+
+        w1_scale_raw = keep.tile([P, H], U8, align_bytes=64)
+        load_scale_rows(nc, w1_scale_raw, w1_scales[0])
+        w1_raw = keep.tile([P, H], I32, align_bytes=64)
+        nc.sync.dma_start(out=w1_raw[:], in_=w1_words[0].rearrange("p i d -> p (i d)").bitcast(I32))
+        x_code = keep.tile([P, T], I32, align_bytes=64)
+        nc.sync.dma_start(out=x_code[:], in_=x_words[0].rearrange("p t d -> p (t d)").bitcast(I32))
+        x_scale = keep.tile([P, T], U8, align_bytes=64)
+        load_scale_rows(nc, x_scale, x_scales[0])
+        slot_token = keep.tile([P, S // 16], U16)
+        nc.sync.dma_start(slot_token[:], offs)
+
+        w2_raw = {}
+
+        def load_w2(half):
+            for e in range(E):
+                raw = keep.tile(
+                    [P, PACK, HALF], F32, align_bytes=64, name=f"w2_raw_{e}_{half}", tag=f"w2_raw_{e}_{half}"
+                )
+                nc.sync.dma_start(
+                    out=raw[:],
+                    in_=w2[e].rearrange("(p j) n -> p j n", j=PACK)[:, :, half * HALF : (half + 1) * HALF],
+                )
+                w2_raw[e, half] = raw
+
+        load_w2(0)
+        token_slot = []
+        gates = []
+        for r, pos in enumerate((pos1, pos2)):
+            lst = keep.tile([P, T // 16], U16, name=f"token_slot_{r}")
+            nc.sync.dma_start(lst[:], pos)
+            token_slot.append(lst)
+        for r in range(2):
+            g = keep.tile([P, T], F32, name=f"gate_{r}")
+            nc.sync.dma_start(out=g[:], in_=gate[r])
+            gates.append(g)
+        load_w2(1)
+
+        w1_scale = keep.tile([P, H], U8, align_bytes=64)
+        nc.vector.tensor_copy(
+            out=w1_scale[:].rearrange("p (t m) -> p t m", t=PACK),
+            in_=w1_scale_raw[:].rearrange("p (m t) -> p t m", t=PACK),
+        )
+        w1_code = keep.tile([P, H], I32, align_bytes=64)
+        nc.vector.tensor_copy(
+            out=w1_code[:].rearrange("p (t m) -> p t m", t=PACK),
+            in_=w1_raw[:].rearrange("p (m t) -> p t m", t=PACK),
+        )
+        h_pairs = []
+        for u in range(2):
+            pairs = keep.tile([P, T], U32, name=f"h_pairs_{u}")
+            for t0 in range(0, T, TOK):
+                bank = psum.tile([P, 2, TOK], F32, tag=f"bank_{3 * u + t0 // TOK}", name="bank1")
+                for v in range(2):
+                    cols = slice((2 * u + v) * P, (2 * u + v + 1) * P)
+                    nc.tensor.matmul_mx(
+                        out=bank[:, v, :],
+                        lhsT=w1_code[:, cols].bitcast(FP8X4),
+                        lhsT_scale=w1_scale[:, cols],
+                        rhs=x_code[:, t0 : t0 + TOK].bitcast(FP8X4),
+                        rhs_scale=x_scale[:, t0 : t0 + TOK],
+                        start=True,
+                        stop=True,
+                    )
+                nc.scalar.activation(
+                    out=pairs[:, t0 : t0 + TOK].bitcast(BF16).rearrange("p (n v) -> p n v", v=2),
+                    in_=bank[:].rearrange("p v n -> p n v"),
+                    func=GELU,
+                )
+            h_pairs.append(pairs)
+
+        groups = {0: ((0, 2), (2, E)), 1: ((0, 4), (4, E)), 2: ((0, 2), (2, E)), 3: ((0, 2), (2, E))}
+        w2_grouped, w2_code = {}, {}
+        w2_scale = [keep.tile([P, E * P], U8, align_bytes=64, name=f"w2_scale_{b}") for b in range(NB)]
+
+        def round_w2(b, e, copy, tag=None):
+            if (b, e) not in w2_grouped:
+                lo, hi = [g for g in groups[b] if g[0] <= e < g[1]][0]
+                name = f"w2_grouped_{b}_{lo}"
+                grp = keep.tile([P, hi - lo, P * PACK], BF16, align_bytes=64, name=name, tag=tag or name)
+                for member in range(lo, hi):
+                    w2_grouped[b, member] = (grp, member - lo)
+            grp, k = w2_grouped[b, e]
+            src = w2_raw[e, b // 2][:, :, (b % 2) * P : (b % 2 + 1) * P]
+            copy(
+                out=grp[:, k, :].rearrange("p (c i j) -> p c j i", i=4, j=PACK),
+                in_=src.rearrange("p j (c i) -> p c j i", i=4),
+            )
+
+        def quantise_w2(b, g, tag):
+            if g == 0:
+                w2_code[b] = keep.tile([P, E * P], U32, align_bytes=64, name=f"w2_code_{b}", tag=tag)
+            lo, hi = groups[b][g]
+            nc.vector.quantize_mx(
+                out=w2_code[b][:, lo * P : hi * P].bitcast(FP8X4),
+                scales=w2_scale[b][:, lo * P : hi * P],
+                in_=w2_grouped[b, lo][0][:].rearrange("p e w -> p (e w)"),
+            )
+
+        h_code, h_scale, picked, grouped = [], [], {}, {}
+        for s in range(S // PIECE):
+            h_code.append(keep.tile([P, PIECE], U32, align_bytes=64, name=f"h_code_{s}"))
+            h_scale.append(keep.tile([P, PIECE], U8, align_bytes=64, name=f"h_scale_{s}"))
+
+        def gather_h(s, u, tag):
+            if u == 0:
+                picked[s] = keep.tile([P, 2, PIECE], U32, align_bytes=64, name=f"picked_{s}", tag=tag)
+            cols = slice(s * PIECE // 16, (s + 1) * PIECE // 16)
+            nc.vector.tensor_copy(out=picked[s][:, u, :], in_=h_pairs[u][:].indirect(slot_token[:, cols]))
+
+        def weave_h(s, copy, word):
+            grouped[s] = keep.tile([P, PIECE * PACK], BF16, align_bytes=64, name=f"h_grouped_{s}", tag=f"h_grouped_{s}")
+            copy(
+                out=grouped[s][:].bitcast(word).rearrange("p (n u) -> p n u", u=2),
+                in_=picked[s][:].bitcast(word).rearrange("p u n -> p n u"),
+            )
+
+        def quantise_h(s):
+            nc.vector.quantize_mx(out=h_code[s][:].bitcast(FP8X4), scales=h_scale[s][:], in_=grouped[s][:])
+
+        y = [keep.tile([P, S], F32, name=f"y_{b}") for b in range(NB)]
+
+        def experts(b):
+            for s in range(S // PIECE):
+                bank = psum.tile([P, PIECE], F32, tag=f"bank_{3 * (b % 2) + s}", name="bank2")
+                for v in range(2):
+                    e = 2 * s + v
+                    nc.tensor.matmul_mx(
+                        out=bank[:, v * C : (v + 1) * C],
+                        lhsT=w2_code[b][:, e * P : (e + 1) * P].bitcast(FP8X4),
+                        lhsT_scale=w2_scale[b][:, e * P : (e + 1) * P],
+                        rhs=h_code[s][:, v * C : (v + 1) * C].bitcast(FP8X4),
+                        rhs_scale=h_scale[s][:, v * C : (v + 1) * C],
+                        start=True,
+                        stop=True,
+                    )
+                nc.scalar.copy(out=y[b][:, s * PIECE : (s + 1) * PIECE], in_=bank[:])
+
+        terms = {}
+
+        def fetch(b, r, lo, hi, tag):
+            term = keep.tile([P, hi - lo], F32, align_bytes=64, name=f"term_{b}_{r}_{lo}", tag=tag)
+            picked_y = y[b][:].indirect(token_slot[r][:, lo // 16 : hi // 16])
+            nc.vector.tensor_tensor(term[:], picked_y, gates[r][:, lo:hi], MULT)
+            terms[b, r, lo] = term
+
+        def add_and_store(b, lo, hi):
+            total = keep.tile([P, hi - lo], F32, name=f"total_{b}_{lo}")
+            nc.vector.tensor_tensor(total[:], terms[b, 0, lo][:], terms[b, 1, lo][:], ADD)
+            nc.sync.dma_start(out=out[b * P : (b + 1) * P, lo:hi], in_=total[:])
+
+        ident = keep.tile([P, P], F32)
+        make_identity(nc, ident[:])
+        turned = {}
+
+        def add_turned(b, first):
+            turned[b] = keep.tile([P, T], F32, name=f"turned_{b}")
+            for lo in range(0, T, T // 2):
+                bank = psum.tile([P, T // 2], F32, tag=f"bank_{first + lo // (T // 2)}", name="bank3")
+                for c in range(0, T // 2, P):
+                    for r in range(2):
+                        nc.tensor.matmul(
+                            bank[:, c : c + P],
+                            terms[b, r, 0][:, lo + c : lo + c + P],
+                            ident[:],
+                            start=(r == 0),
+                            stop=(r == 1),
+                            is_transpose=True,
+                        )
+                nc.scalar.copy(out=turned[b][:, lo : lo + T // 2], in_=bank[:])
+
+        def turn_back_and_store(b, first):
+            total = keep.tile([P, T], F32, name=f"total_{b}")
+            for lo in range(0, T, T // 2):
+                bank = psum.tile([P, T // 2], F32, tag=f"bank_{first + lo // (T // 2)}", name="bank4")
+                for c in range(0, T // 2, P):
+                    nc.tensor.transpose(bank[:, c : c + P], turned[b][:, lo + c : lo + c + P], ident[:])
+                nc.scalar.copy(out=total[:, lo : lo + T // 2], in_=bank[:])
+                nc.scalar.dma_start(
+                    out=out[b * P : (b + 1) * P, lo : lo + T // 2], in_=total[:, lo : lo + T // 2]
+                )
+
+        on_vector, on_scalar = nc.vector.tensor_copy, nc.scalar.copy
+        for e in range(2):
+            for b in range(2):
+                round_w2(b, e, on_vector)
+        quantise_w2(0, 0, "w2_code_0")
+        for b in range(2):
+            round_w2(b, 2, on_scalar)
+        gather_h(0, 0, "picked_0")
+        gather_h(1, 0, "picked_1")
+        gather_h(0, 1, None)
+        gather_h(1, 1, None)
+        gather_h(2, 0, "w2_raw_2_0")
+        gather_h(2, 1, None)
+        for e in (3, 4, 5):
+            round_w2(0, e, on_scalar)
+        weave_h(0, on_scalar, U32)
+        weave_h(1, on_scalar, U32)
+        for e in (3, 4):
+            round_w2(1, e, on_scalar)
+        weave_h(2, on_scalar, U32)
+        round_w2(1, 5, on_scalar)
+        quantise_w2(0, 1, None)
+        quantise_h(0)
+        quantise_h(1)
+        quantise_h(2)
+        quantise_w2(1, 0, "w2_raw_2_0")
+        quantise_w2(1, 1, None)
+        for e in range(2):
+            round_w2(2, e, on_vector, "h_grouped_2")
+        quantise_w2(2, 0, "w2_code_2")
+        experts(0)
+        experts(1)
+        for e in range(2, E):
+            round_w2(2, e, on_scalar)
+        for e in range(E):
+            round_w2(3, e, on_scalar)
+        fetch(0, 0, 0, T, "term_a")
+        fetch(0, 1, 0, T, "term_b")
+        quantise_w2(2, 1, None)
+        experts(2)
+        fetch(1, 0, 0, T, "w2_grouped_2_2")
+        fetch(1, 1, 0, T, "term_c")
+        quantise_w2(3, 0, "w2_code_3")
+        quantise_w2(3, 1, None)
+        add_turned(0, 6)
+        experts(3)
+        fetch(2, 0, 0, T, "term_d")
+        fetch(2, 1, 0, T, "term_e")
+        add_turned(1, 0)
+        turn_back_and_store(0, 6)
+        turn_back_and_store(1, 3)
+        add_turned(2, 6)
+        turn_back_and_store(2, 0)
+        cut = 512
+        fetch(3, 0, 0, cut, "term_f")
+        fetch(3, 1, 0, cut, "term_g")
+        fetch(3, 0, cut, T, "term_h")
+        add_and_store(3, 0, cut)
+        fetch(3, 1, cut, T, "term_i")
+        add_and_store(3, cut, T)

@@ -26,14 +26,10 @@ TOK = 256
 PIECE = 2 * C
 
 
-def load_scale_rows(nc, plane, rows):
-    width = rows.shape[1] // 4
+def load_scale_rows(nc, plane, rows, which):
     by_row = rows.bitcast(I32).rearrange("(q r) w -> r q w", r=4)
-    for r in range(4):
-        nc.sync.dma_start(
-            out=plane[:].bitcast(I32)[r:P:4, :],
-            in_=by_row[r].unsqueeze(1).broadcast_to([4, 8, width]),
-        )
+    for r in which:
+        nc.sync.dma_start(out=plane[:].bitcast(I32)[r:P:32, :], in_=by_row[r])
 
 
 def tile_moe_sup_lin_gelu_kernel(
@@ -44,21 +40,21 @@ def tile_moe_sup_lin_gelu_kernel(
         keep = ctx.enter_context(tc.tile_pool(name="keep", bufs=1))
         psum = ctx.enter_context(tc.psum_pool(name="psum", bufs=1))
 
+        x_scale = keep.tile([P, T], U8, align_bytes=64)
+        load_scale_rows(nc, x_scale, x_scales[0], range(4))
         w1_scale_raw = keep.tile([P, H], U8, align_bytes=64)
-        load_scale_rows(nc, w1_scale_raw, w1_scales[0])
+        nc.gpsimd.memset(w1_scale_raw[:].bitcast(I32), 0)
+        load_scale_rows(nc, w1_scale_raw, w1_scales[0], (0, 1))
         w1_raw = keep.tile([P, H], I32, align_bytes=64)
         nc.sync.dma_start(out=w1_raw[:], in_=w1_words[0].rearrange("p i d -> p (i d)").bitcast(I32))
         x_code = keep.tile([P, T], I32, align_bytes=64)
         nc.sync.dma_start(out=x_code[:], in_=x_words[0].rearrange("p t d -> p (t d)").bitcast(I32))
-        x_scale = keep.tile([P, T], U8, align_bytes=64)
-        load_scale_rows(nc, x_scale, x_scales[0])
-        slot_token = keep.tile([P, S // 16], U16)
-        nc.sync.dma_start(slot_token[:], offs)
+        load_scale_rows(nc, w1_scale_raw, w1_scales[0], (2, 3))
 
         w2_raw = {}
 
-        def load_w2(half):
-            for e in range(E):
+        def load_w2(half, which):
+            for e in which:
                 raw = keep.tile(
                     [P, PACK, HALF], F32, align_bytes=64, name=f"w2_raw_{e}_{half}", tag=f"w2_raw_{e}_{half}"
                 )
@@ -68,7 +64,10 @@ def tile_moe_sup_lin_gelu_kernel(
                 )
                 w2_raw[e, half] = raw
 
-        load_w2(0)
+        load_w2(0, range(1))
+        slot_token = keep.tile([P, S // 16], U16)
+        nc.sync.dma_start(slot_token[:], offs)
+        load_w2(0, range(1, E))
         token_slot = []
         gates = []
         for r, pos in enumerate((pos1, pos2)):
@@ -79,7 +78,7 @@ def tile_moe_sup_lin_gelu_kernel(
             g = keep.tile([P, T], F32, name=f"gate_{r}")
             nc.sync.dma_start(out=g[:], in_=gate[r])
             gates.append(g)
-        load_w2(1)
+        load_w2(1, range(E))
 
         w1_scale = keep.tile([P, H], U8, align_bytes=64)
         nc.vector.tensor_copy(
@@ -198,15 +197,19 @@ def tile_moe_sup_lin_gelu_kernel(
         make_identity(nc, ident[:])
         turned = {}
 
-        def add_turned(b, first):
-            turned[b] = keep.tile([P, T], F32, name=f"turned_{b}")
-            for lo in range(0, T, T // 2):
+        def term_columns(b, r, col):
+            lo = max(key[2] for key in terms if key[:2] == (b, r) and key[2] <= col)
+            return terms[b, r, lo][:, col - lo : col - lo + P]
+
+        def add_turned(b, first, width):
+            turned[b] = keep.tile([P, width], F32, name=f"turned_{b}")
+            for lo in range(0, width, T // 2):
                 bank = psum.tile([P, T // 2], F32, tag=f"bank_{first + lo // (T // 2)}", name="bank3")
                 for c in range(0, T // 2, P):
                     for r in range(2):
                         nc.tensor.matmul(
                             bank[:, c : c + P],
-                            terms[b, r, 0][:, lo + c : lo + c + P],
+                            term_columns(b, r, lo + c),
                             ident[:],
                             start=(r == 0),
                             stop=(r == 1),
@@ -214,9 +217,9 @@ def tile_moe_sup_lin_gelu_kernel(
                         )
                 nc.scalar.copy(out=turned[b][:, lo : lo + T // 2], in_=bank[:])
 
-        def turn_back_and_store(b, first):
-            total = keep.tile([P, T], F32, name=f"total_{b}")
-            for lo in range(0, T, T // 2):
+        def turn_back_and_store(b, first, width):
+            total = keep.tile([P, width], F32, name=f"total_{b}")
+            for lo in range(0, width, T // 2):
                 bank = psum.tile([P, T // 2], F32, tag=f"bank_{first + lo // (T // 2)}", name="bank4")
                 for c in range(0, T // 2, P):
                     nc.tensor.transpose(bank[:, c : c + P], turned[b][:, lo + c : lo + c + P], ident[:])
@@ -226,10 +229,11 @@ def tile_moe_sup_lin_gelu_kernel(
                 )
 
         on_vector, on_scalar = nc.vector.tensor_copy, nc.scalar.copy
-        for e in range(2):
-            for b in range(2):
-                round_w2(b, e, on_vector)
+        for b in range(2):
+            round_w2(b, 0, on_vector)
+        round_w2(0, 1, on_vector)
         quantise_w2(0, 0, "w2_code_0")
+        round_w2(1, 1, on_scalar)
         for b in range(2):
             round_w2(b, 2, on_scalar)
         gather_h(0, 0, "picked_0")
@@ -238,48 +242,51 @@ def tile_moe_sup_lin_gelu_kernel(
         gather_h(1, 1, None)
         gather_h(2, 0, "w2_raw_2_0")
         gather_h(2, 1, None)
-        for e in (3, 4, 5):
-            round_w2(0, e, on_scalar)
+        round_w2(0, 3, on_scalar)
         weave_h(0, on_scalar, U32)
+        for e in (4, 5):
+            round_w2(0, e, on_scalar)
         weave_h(1, on_scalar, U32)
-        for e in (3, 4):
-            round_w2(1, e, on_scalar)
         weave_h(2, on_scalar, U32)
-        round_w2(1, 5, on_scalar)
-        quantise_w2(0, 1, None)
+        round_w2(1, 3, on_scalar)
         quantise_h(0)
+        quantise_w2(0, 1, None)
         quantise_h(1)
         quantise_h(2)
+        for e in (4, 5):
+            round_w2(1, e, on_vector, "h_grouped_2")
         quantise_w2(1, 0, "w2_raw_2_0")
-        quantise_w2(1, 1, None)
         for e in range(2):
-            round_w2(2, e, on_vector, "h_grouped_2")
+            round_w2(2, e, on_vector, "h_grouped_1")
+        quantise_w2(1, 1, None)
         quantise_w2(2, 0, "w2_code_2")
         experts(0)
         experts(1)
         for e in range(2, E):
-            round_w2(2, e, on_scalar)
+            round_w2(2, e, on_scalar, "w2_code_0")
         for e in range(E):
-            round_w2(3, e, on_scalar)
+            round_w2(3, e, on_scalar, "h_grouped_0" if e < 2 else None)
         fetch(0, 0, 0, T, "term_a")
         fetch(0, 1, 0, T, "term_b")
+        fetch(1, 0, 0, T, "term_c")
         quantise_w2(2, 1, None)
         experts(2)
-        fetch(1, 0, 0, T, "w2_grouped_2_2")
-        fetch(1, 1, 0, T, "term_c")
+        fetch(1, 1, 0, T, "w2_code_0")
         quantise_w2(3, 0, "w2_code_3")
         quantise_w2(3, 1, None)
-        add_turned(0, 6)
+        add_turned(0, 6, T)
         experts(3)
-        fetch(2, 0, 0, T, "term_d")
-        fetch(2, 1, 0, T, "term_e")
-        add_turned(1, 0)
-        turn_back_and_store(0, 6)
-        turn_back_and_store(1, 3)
-        add_turned(2, 6)
-        turn_back_and_store(2, 0)
+        for lo in (0, T // 2):
+            for r in range(2):
+                fetch(2, r, lo, lo + T // 2, f"term_2_{r}_{lo}")
+        add_turned(1, 0, T)
+        turn_back_and_store(0, 6, T)
+        add_turned(2, 2, T // 2)
+        turn_back_and_store(1, 3, T)
+        turn_back_and_store(2, 5, T // 2)
         cut = 512
         fetch(3, 0, 0, cut, "term_f")
+        add_and_store(2, T // 2, T)
         fetch(3, 1, 0, cut, "term_g")
         fetch(3, 0, cut, T, "term_h")
         add_and_store(3, 0, cut)

@@ -40,16 +40,19 @@ def tile_moe_sup_lin_gelu_kernel(
         keep = ctx.enter_context(tc.tile_pool(name="keep", bufs=1))
         psum = ctx.enter_context(tc.psum_pool(name="psum", bufs=1))
 
-        x_scale = keep.tile([P, T], U8, align_bytes=64)
-        load_scale_rows(nc, x_scale, x_scales[0], range(4))
         w1_scale_raw = keep.tile([P, H], U8, align_bytes=64)
-        nc.gpsimd.memset(w1_scale_raw[:].bitcast(I32), 0)
-        load_scale_rows(nc, w1_scale_raw, w1_scales[0], (0, 1))
+        rows = w1_scales[0].bitcast(I32)
+        for q in range(4):
+            nc.sync.dma_start(
+                out=w1_scale_raw[:].bitcast(I32)[32 * q : 32 * (q + 1), :],
+                in_=rows[4 * q : 4 * (q + 1), :].unsqueeze(0).broadcast_to([8, 4, H // 4]),
+            )
         w1_raw = keep.tile([P, H], I32, align_bytes=64)
         nc.sync.dma_start(out=w1_raw[:], in_=w1_words[0].rearrange("p i d -> p (i d)").bitcast(I32))
         x_code = keep.tile([P, T], I32, align_bytes=64)
         nc.sync.dma_start(out=x_code[:], in_=x_words[0].rearrange("p t d -> p (t d)").bitcast(I32))
-        load_scale_rows(nc, w1_scale_raw, w1_scales[0], (2, 3))
+        x_scale = keep.tile([P, T], U8, align_bytes=64)
+        load_scale_rows(nc, x_scale, x_scales[0], range(4))
 
         w2_raw = {}
 
@@ -68,6 +71,7 @@ def tile_moe_sup_lin_gelu_kernel(
         slot_token = keep.tile([P, S // 16], U16)
         nc.sync.dma_start(slot_token[:], offs)
         load_w2(0, range(1, E))
+        load_w2(1, range(2))
         token_slot = []
         gates = []
         for r, pos in enumerate((pos1, pos2)):
@@ -78,7 +82,7 @@ def tile_moe_sup_lin_gelu_kernel(
             g = keep.tile([P, T], F32, name=f"gate_{r}")
             nc.sync.dma_start(out=g[:], in_=gate[r])
             gates.append(g)
-        load_w2(1, range(E))
+        load_w2(1, range(2, E))
 
         w1_scale = keep.tile([P, H], U8, align_bytes=64)
         nc.vector.tensor_copy(
@@ -113,9 +117,9 @@ def tile_moe_sup_lin_gelu_kernel(
                 )
             h_pairs.append(pairs)
 
-        groups = {0: ((0, 2), (2, E)), 1: ((0, 4), (4, E)), 2: ((0, 2), (2, E)), 3: ((0, 2), (2, E))}
+        groups = {0: ((0, 1), (1, 5), (5, E)), 1: ((0, 1), (1, 5), (5, E)), 2: ((0, 2), (2, E)), 3: ((0, 2), (2, E))}
         w2_grouped, w2_code = {}, {}
-        w2_scale = [keep.tile([P, E * P], U8, align_bytes=64, name=f"w2_scale_{b}") for b in range(NB)]
+        w2_scale = [keep.tile([P, E * P], U8, align_bytes=64, name=f"w2_scale_{b}", tag=f"w2_scale_{b}") for b in range(NB)]
 
         def round_w2(b, e, copy, tag=None):
             if (b, e) not in w2_grouped:
@@ -126,17 +130,26 @@ def tile_moe_sup_lin_gelu_kernel(
                     w2_grouped[b, member] = (grp, member - lo)
             grp, k = w2_grouped[b, e]
             src = w2_raw[e, b // 2][:, :, (b % 2) * P : (b % 2 + 1) * P]
-            copy(
-                out=grp[:, k, :].rearrange("p (c i j) -> p c j i", i=4, j=PACK),
-                in_=src.rearrange("p j (c i) -> p c j i", i=4),
-            )
+            if copy is on_gpsimd:
+                copy(out=grp[:, k, :].rearrange("p (n j) -> p n j", j=PACK), in_=src.rearrange("p j n -> p n j"))
+            else:
+                copy(
+                    out=grp[:, k, :].rearrange("p (c i j) -> p c j i", i=4, j=PACK),
+                    in_=src.rearrange("p j (c i) -> p c j i", i=4),
+                )
+
+        def on_gpsimd(out, in_):
+            nc.gpsimd.tensor_scalar(out, in_, 1.0, 0.0, MULT, ADD)
 
         def quantise_w2(b, g, tag):
-            if g == 0:
-                w2_code[b] = keep.tile([P, E * P], U32, align_bytes=64, name=f"w2_code_{b}", tag=tag)
             lo, hi = groups[b][g]
+            if tag is not None:
+                code = keep.tile([P, (E - lo) * P], U32, align_bytes=64, name=f"w2_code_{b}_{lo}", tag=tag)
+                for e in range(lo, E):
+                    w2_code[b, e] = (code, e - lo)
+            code, k = w2_code[b, lo]
             nc.vector.quantize_mx(
-                out=w2_code[b][:, lo * P : hi * P].bitcast(FP8X4),
+                out=code[:, k * P : (k + hi - lo) * P].bitcast(FP8X4),
                 scales=w2_scale[b][:, lo * P : hi * P],
                 in_=w2_grouped[b, lo][0][:].rearrange("p e w -> p (e w)"),
             )
@@ -169,9 +182,10 @@ def tile_moe_sup_lin_gelu_kernel(
                 bank = psum.tile([P, PIECE], F32, tag=f"bank_{3 * (b % 2) + s}", name="bank2")
                 for v in range(2):
                     e = 2 * s + v
+                    code, k = w2_code[b, e]
                     nc.tensor.matmul_mx(
                         out=bank[:, v * C : (v + 1) * C],
-                        lhsT=w2_code[b][:, e * P : (e + 1) * P].bitcast(FP8X4),
+                        lhsT=code[:, k * P : (k + 1) * P].bitcast(FP8X4),
                         lhsT_scale=w2_scale[b][:, e * P : (e + 1) * P],
                         rhs=h_code[s][:, v * C : (v + 1) * C].bitcast(FP8X4),
                         rhs_scale=h_scale[s][:, v * C : (v + 1) * C],
@@ -231,62 +245,62 @@ def tile_moe_sup_lin_gelu_kernel(
         on_vector, on_scalar = nc.vector.tensor_copy, nc.scalar.copy
         for b in range(2):
             round_w2(b, 0, on_vector)
-        round_w2(0, 1, on_vector)
-        quantise_w2(0, 0, "w2_code_0")
-        round_w2(1, 1, on_scalar)
         for b in range(2):
-            round_w2(b, 2, on_scalar)
+            quantise_w2(b, 0, f"w2_code_{b}")
+        for e in range(1, E):
+            round_w2(1, e, on_gpsimd)
+        round_w2(2, 0, on_gpsimd)
+        for e in (1, 2):
+            round_w2(0, e, on_scalar)
         gather_h(0, 0, "picked_0")
         gather_h(1, 0, "picked_1")
         gather_h(0, 1, None)
         gather_h(1, 1, None)
         gather_h(2, 0, "w2_raw_2_0")
         gather_h(2, 1, None)
-        round_w2(0, 3, on_scalar)
-        weave_h(0, on_scalar, U32)
-        for e in (4, 5):
+        for e in (3, 4):
             round_w2(0, e, on_scalar)
+        weave_h(0, on_scalar, U32)
+        round_w2(0, 5, on_scalar)
         weave_h(1, on_scalar, U32)
         weave_h(2, on_scalar, U32)
-        round_w2(1, 3, on_scalar)
+        round_w2(2, 1, on_scalar)
         quantise_h(0)
         quantise_w2(0, 1, None)
+        quantise_w2(0, 2, "w2_code_0_5")
         quantise_h(1)
         quantise_h(2)
-        for e in (4, 5):
-            round_w2(1, e, on_vector, "h_grouped_2")
-        quantise_w2(1, 0, "w2_raw_2_0")
+        quantise_w2(1, 1, "w2_raw_2_0")
+        quantise_w2(1, 2, None)
         for e in range(2):
-            round_w2(2, e, on_vector, "h_grouped_1")
-        quantise_w2(1, 1, None)
+            round_w2(3, e, on_vector, "h_grouped_2")
         quantise_w2(2, 0, "w2_code_2")
+        quantise_w2(3, 0, "w2_code_3")
         experts(0)
         experts(1)
         for e in range(2, E):
-            round_w2(2, e, on_scalar, "w2_code_0")
-        for e in range(E):
-            round_w2(3, e, on_scalar, "h_grouped_0" if e < 2 else None)
+            round_w2(2, e, on_scalar, "w2_code_0_5")
+        for e in range(2, E):
+            round_w2(3, e, on_scalar, "w2_scale_0")
         fetch(0, 0, 0, T, "term_a")
         fetch(0, 1, 0, T, "term_b")
         fetch(1, 0, 0, T, "term_c")
         quantise_w2(2, 1, None)
-        experts(2)
-        fetch(1, 1, 0, T, "w2_code_0")
-        quantise_w2(3, 0, "w2_code_3")
-        quantise_w2(3, 1, None)
         add_turned(0, 6, T)
+        experts(2)
+        fetch(1, 1, 0, T, "w2_code_0_5")
+        quantise_w2(3, 1, None)
+        turn_back_and_store(0, 6, T)
         experts(3)
         for lo in (0, T // 2):
             for r in range(2):
                 fetch(2, r, lo, lo + T // 2, f"term_2_{r}_{lo}")
         add_turned(1, 0, T)
-        turn_back_and_store(0, 6, T)
-        add_turned(2, 2, T // 2)
-        turn_back_and_store(1, 3, T)
-        turn_back_and_store(2, 5, T // 2)
+        turn_back_and_store(1, 6, T)
+        add_turned(2, 3, T)
+        turn_back_and_store(2, 0, T)
         cut = 512
         fetch(3, 0, 0, cut, "term_f")
-        add_and_store(2, T // 2, T)
         fetch(3, 1, 0, cut, "term_g")
         fetch(3, 0, cut, T, "term_h")
         add_and_store(3, 0, cut)

@@ -56,22 +56,20 @@ def tile_moe_sup_lin_gelu_kernel(
 
         w2_raw = {}
 
-        def load_w2(half, which):
-            for e in which:
-                raw = keep.tile(
-                    [P, PACK, HALF], F32, align_bytes=64, name=f"w2_raw_{e}_{half}", tag=f"w2_raw_{e}_{half}"
-                )
-                nc.sync.dma_start(
-                    out=raw[:],
-                    in_=w2[e].rearrange("(p j) n -> p j n", j=PACK)[:, :, half * HALF : (half + 1) * HALF],
-                )
-                w2_raw[e, half] = raw
+        def load_w2(e, lo, hi):
+            name = f"w2_raw_{e}_{lo}"
+            raw = keep.tile([P, PACK, hi - lo], F32, align_bytes=64, name=name, tag=name)
+            nc.sync.dma_start(out=raw[:], in_=w2[e].rearrange("(p j) n -> p j n", j=PACK)[:, :, lo:hi])
+            for b in range(lo // P, hi // P):
+                w2_raw[e, b] = raw[:, :, b * P - lo : (b + 1) * P - lo]
 
-        load_w2(0, range(1))
+        load_w2(0, 0, HALF)
         slot_token = keep.tile([P, S // 16], U16)
         nc.sync.dma_start(slot_token[:], offs)
-        load_w2(0, range(1, E))
-        load_w2(1, range(2))
+        for e in (1, 2, 3):
+            load_w2(e, 0, N)
+        for e in (4, 5):
+            load_w2(e, 0, HALF)
         token_slot = []
         gates = []
         for r, pos in enumerate((pos1, pos2)):
@@ -82,7 +80,8 @@ def tile_moe_sup_lin_gelu_kernel(
             g = keep.tile([P, T], F32, name=f"gate_{r}")
             nc.sync.dma_start(out=g[:], in_=gate[r])
             gates.append(g)
-        load_w2(1, range(2, E))
+        for e in (0, 4, 5):
+            load_w2(e, HALF, N)
 
         w1_scale = keep.tile([P, H], U8, align_bytes=64)
         nc.vector.tensor_copy(
@@ -117,42 +116,44 @@ def tile_moe_sup_lin_gelu_kernel(
                 )
             h_pairs.append(pairs)
 
-        groups = {0: ((0, 1), (1, 5), (5, E)), 1: ((0, 1), (1, 5), (5, E)), 2: ((0, 2), (2, E)), 3: ((0, 2), (2, E))}
-        w2_grouped, w2_code = {}, {}
-        w2_scale = [keep.tile([P, E * P], U8, align_bytes=64, name=f"w2_scale_{b}", tag=f"w2_scale_{b}") for b in range(NB)]
+        early = ((0,), (1, 2, 3, 4), (5,))
+        late = ((1, 2), (3, 0, 4, 5))
+        groups = (early, early, ((1, 2), (3,), (0, 4), (5,)), late)
+        w2_grouped, w2_code, w2_scale = {}, {}, {}
 
         def round_w2(b, e, copy, tag=None):
-            if (b, e) not in w2_grouped:
-                lo, hi = [g for g in groups[b] if g[0] <= e < g[1]][0]
-                name = f"w2_grouped_{b}_{lo}"
-                grp = keep.tile([P, hi - lo, P * PACK], BF16, align_bytes=64, name=name, tag=tag or name)
-                for member in range(lo, hi):
-                    w2_grouped[b, member] = (grp, member - lo)
-            grp, k = w2_grouped[b, e]
-            src = w2_raw[e, b // 2][:, :, (b % 2) * P : (b % 2 + 1) * P]
+            group = [g for g in groups[b] if e in g][0]
+            if (b, group) not in w2_grouped:
+                name = f"w2_grouped_{b}_{group[0]}"
+                w2_grouped[b, group] = keep.tile(
+                    [P, len(group), P * PACK], BF16, align_bytes=64, name=name, tag=tag or name
+                )
+            dst, src = w2_grouped[b, group][:, group.index(e), :], w2_raw[e, b]
             if copy is on_gpsimd:
-                copy(out=grp[:, k, :].rearrange("p (n j) -> p n j", j=PACK), in_=src.rearrange("p j n -> p n j"))
+                copy(out=dst.rearrange("p (n j) -> p n j", j=PACK), in_=src.rearrange("p j n -> p n j"))
             else:
                 copy(
-                    out=grp[:, k, :].rearrange("p (c i j) -> p c j i", i=4, j=PACK),
+                    out=dst.rearrange("p (c i j) -> p c j i", i=4, j=PACK),
                     in_=src.rearrange("p j (c i) -> p c j i", i=4),
                 )
 
         def on_gpsimd(out, in_):
             nc.gpsimd.tensor_scalar(out, in_, 1.0, 0.0, MULT, ADD)
 
-        def quantise_w2(b, g, tag):
-            lo, hi = groups[b][g]
-            if tag is not None:
-                code = keep.tile([P, (E - lo) * P], U32, align_bytes=64, name=f"w2_code_{b}_{lo}", tag=tag)
-                for e in range(lo, E):
-                    w2_code[b, e] = (code, e - lo)
-            code, k = w2_code[b, lo]
+        def quantise_w2(b, g, tag=None):
+            group = groups[b][g]
+            name = f"w2_code_{b}_{g}"
+            code = keep.tile([P, len(group) * P], U32, align_bytes=64, name=name, tag=tag or name)
+            name = f"w2_scale_{b}_{g}"
+            scale = keep.tile([P, len(group) * P], U8, align_bytes=64, name=name, tag=name)
             nc.vector.quantize_mx(
-                out=code[:, k * P : (k + hi - lo) * P].bitcast(FP8X4),
-                scales=w2_scale[b][:, lo * P : hi * P],
-                in_=w2_grouped[b, lo][0][:].rearrange("p e w -> p (e w)"),
+                out=code[:].bitcast(FP8X4),
+                scales=scale[:],
+                in_=w2_grouped[b, group][:].rearrange("p e w -> p (e w)"),
             )
+            for k, e in enumerate(group):
+                w2_code[b, e] = code[:, k * P : (k + 1) * P]
+                w2_scale[b, e] = scale[:, k * P : (k + 1) * P]
 
         h_code, h_scale, picked, grouped = [], [], {}, {}
         for s in range(S // PIECE):
@@ -182,11 +183,10 @@ def tile_moe_sup_lin_gelu_kernel(
                 bank = psum.tile([P, PIECE], F32, tag=f"bank_{3 * (b % 2) + s}", name="bank2")
                 for v in range(2):
                     e = 2 * s + v
-                    code, k = w2_code[b, e]
                     nc.tensor.matmul_mx(
                         out=bank[:, v * C : (v + 1) * C],
-                        lhsT=code[:, k * P : (k + 1) * P].bitcast(FP8X4),
-                        lhsT_scale=w2_scale[b][:, e * P : (e + 1) * P],
+                        lhsT=w2_code[b, e].bitcast(FP8X4),
+                        lhsT_scale=w2_scale[b, e],
                         rhs=h_code[s][:, v * C : (v + 1) * C].bitcast(FP8X4),
                         rhs_scale=h_scale[s][:, v * C : (v + 1) * C],
                         start=True,
@@ -218,7 +218,7 @@ def tile_moe_sup_lin_gelu_kernel(
         def add_turned(b, first, width):
             turned[b] = keep.tile([P, width], F32, name=f"turned_{b}")
             for lo in range(0, width, T // 2):
-                bank = psum.tile([P, T // 2], F32, tag=f"bank_{first + lo // (T // 2)}", name="bank3")
+                bank = psum.tile([P, T // 2], F32, tag=f"bank_{first[lo // (T // 2)]}", name="bank3")
                 for c in range(0, T // 2, P):
                     for r in range(2):
                         nc.tensor.matmul(
@@ -234,7 +234,7 @@ def tile_moe_sup_lin_gelu_kernel(
         def turn_back_and_store(b, first, width):
             total = keep.tile([P, width], F32, name=f"total_{b}")
             for lo in range(0, width, T // 2):
-                bank = psum.tile([P, T // 2], F32, tag=f"bank_{first + lo // (T // 2)}", name="bank4")
+                bank = psum.tile([P, T // 2], F32, tag=f"bank_{first[lo // (T // 2)]}", name="bank4")
                 for c in range(0, T // 2, P):
                     nc.tensor.transpose(bank[:, c : c + P], turned[b][:, lo + c : lo + c + P], ident[:])
                 nc.scalar.copy(out=total[:, lo : lo + T // 2], in_=bank[:])
@@ -246,59 +246,63 @@ def tile_moe_sup_lin_gelu_kernel(
         for b in range(2):
             round_w2(b, 0, on_vector)
         for b in range(2):
-            quantise_w2(b, 0, f"w2_code_{b}")
-        for e in range(1, E):
-            round_w2(1, e, on_gpsimd)
-        round_w2(2, 0, on_gpsimd)
-        for e in (1, 2):
-            round_w2(0, e, on_scalar)
+            quantise_w2(b, 0)
+        for b, e in ((3, 1), (2, 2), (3, 2), (2, 3)):
+            round_w2(b, e, on_gpsimd)
+        for b in range(3):
+            round_w2(b, 1, on_scalar)
         gather_h(0, 0, "picked_0")
         gather_h(1, 0, "picked_1")
         gather_h(0, 1, None)
         gather_h(1, 1, None)
-        gather_h(2, 0, "w2_raw_2_0")
+        gather_h(2, 0, "w2_raw_1_0")
         gather_h(2, 1, None)
-        for e in (3, 4):
-            round_w2(0, e, on_scalar)
+        round_w2(0, 2, on_scalar)
         weave_h(0, on_scalar, U32)
-        round_w2(0, 5, on_scalar)
+        round_w2(1, 2, on_scalar)
+        round_w2(0, 3, on_scalar)
         weave_h(1, on_scalar, U32)
         weave_h(2, on_scalar, U32)
-        round_w2(2, 1, on_scalar)
+        for e in (3, 4):
+            round_w2(1, e, on_scalar)
         quantise_h(0)
-        quantise_w2(0, 1, None)
-        quantise_w2(0, 2, "w2_code_0_5")
+        round_w2(0, 4, on_vector)
         quantise_h(1)
+        quantise_w2(0, 1)
+        round_w2(0, 5, on_vector)
         quantise_h(2)
-        quantise_w2(1, 1, "w2_raw_2_0")
-        quantise_w2(1, 2, None)
-        for e in range(2):
-            round_w2(3, e, on_vector, "h_grouped_2")
-        quantise_w2(2, 0, "w2_code_2")
-        quantise_w2(3, 0, "w2_code_3")
+        quantise_w2(0, 2)
+        round_w2(1, 5, on_vector, "h_grouped_2")
+        quantise_w2(1, 1, "w2_raw_1_0")
+        quantise_w2(1, 2)
         experts(0)
+        quantise_w2(2, 0, "w2_scale_0_1")
+        quantise_w2(3, 0, "w2_code_0_1")
         experts(1)
-        for e in range(2, E):
-            round_w2(2, e, on_scalar, "w2_code_0_5")
-        for e in range(2, E):
-            round_w2(3, e, on_scalar, "w2_scale_0")
+        quantise_w2(2, 1, "h_grouped_2")
+        for e in (0, 4):
+            round_w2(2, e, on_scalar, "w2_code_0_2")
+        round_w2(2, 5, on_scalar)
+        for e in (3, 0, 4, 5):
+            round_w2(3, e, on_scalar, "w2_scale_0_2")
         fetch(0, 0, 0, T, "term_a")
         fetch(0, 1, 0, T, "term_b")
         fetch(1, 0, 0, T, "term_c")
-        quantise_w2(2, 1, None)
-        add_turned(0, 6, T)
+        quantise_w2(2, 2)
+        quantise_w2(2, 3)
+        add_turned(0, (6, 7), T)
         experts(2)
-        fetch(1, 1, 0, T, "w2_code_0_5")
-        quantise_w2(3, 1, None)
-        turn_back_and_store(0, 6, T)
+        fetch(1, 1, 0, T, "w2_grouped_2_5")
+        quantise_w2(3, 1)
+        turn_back_and_store(0, (6, 7), T)
         experts(3)
         for lo in (0, T // 2):
             for r in range(2):
                 fetch(2, r, lo, lo + T // 2, f"term_2_{r}_{lo}")
-        add_turned(1, 0, T)
-        turn_back_and_store(1, 6, T)
-        add_turned(2, 3, T)
-        turn_back_and_store(2, 0, T)
+        add_turned(1, (0, 1), T)
+        turn_back_and_store(1, (6, 7), T)
+        add_turned(2, (3, 1), T)
+        turn_back_and_store(2, (4, 5), T)
         cut = 512
         fetch(3, 0, 0, cut, "term_f")
         fetch(3, 1, 0, cut, "term_g")

from contextlib import ExitStack

import concourse.mybir as mybir
from concourse.masks import make_identity

K, T, E, C, H, N = 512, 768, 6, 256, 512, 512
S = E * C
P = 128
PACK = 4
FLOPS = 2 * K * H * T + 2 * H * N * S

F32 = mybir.dt.float32
BF16 = mybir.dt.bfloat16
I32 = mybir.dt.int32
U32 = mybir.dt.uint32
U16 = mybir.dt.uint16
U8 = mybir.dt.uint8
FP8X4 = mybir.dt.float8_e4m3fn_x4
GELU = mybir.ActivationFunctionType.Gelu_apprx_tanh
MULT = mybir.AluOpType.mult
ADD = mybir.AluOpType.add

NB = N // P
HALF = N // 2
TOK = 256
PIECE = 2 * C


def load_scale_rows(nc, plane, rows, which):
    by_row = rows.bitcast(I32).rearrange("(q r) w -> r q w", r=4)
    for r in which:
        nc.sync.dma_start(out=plane[:].bitcast(I32)[r:P:32, :], in_=by_row[r])


def tile_moe_sup_lin_gelu_kernel(
    tc, x_words, x_scales, w1_words, w1_scales, w2, gate, offs, pos1, pos2, out
):
    nc = tc.nc
    with ExitStack() as ctx:
        keep = ctx.enter_context(tc.tile_pool(name="keep", bufs=1))
        psum = ctx.enter_context(tc.psum_pool(name="psum", bufs=1))

        w1_scale_raw = keep.tile([P, H], U8, align_bytes=64)
        rows = w1_scales[0].bitcast(I32)
        for q in range(4):
            nc.sync.dma_start(
                out=w1_scale_raw[:].bitcast(I32)[32 * q : 32 * (q + 1), :],
                in_=rows[4 * q : 4 * (q + 1), :].unsqueeze(0).broadcast_to([8, 4, H // 4]),
            )
        w1_raw = keep.tile([P, H], I32, align_bytes=64)
        nc.sync.dma_start(out=w1_raw[:], in_=w1_words[0].rearrange("p i d -> p (i d)").bitcast(I32))
        x_code = keep.tile([P, T], I32, align_bytes=64)
        nc.sync.dma_start(out=x_code[:], in_=x_words[0].rearrange("p t d -> p (t d)").bitcast(I32))
        x_scale = keep.tile([P, T], U8, align_bytes=64)
        load_scale_rows(nc, x_scale, x_scales[0], range(4))

        w2_raw = {}

        def load_w2(e, lo, hi):
            name = f"w2_raw_{e}_{lo}"
            raw = keep.tile([P, PACK, hi - lo], F32, align_bytes=64, name=name, tag=name)
            nc.sync.dma_start(out=raw[:], in_=w2[e].rearrange("(p j) n -> p j n", j=PACK)[:, :, lo:hi])
            for b in range(lo // P, hi // P):
                w2_raw[e, b] = raw[:, :, b * P - lo : (b + 1) * P - lo]

        load_w2(0, 0, HALF)
        slot_token = keep.tile([P, S // 16], U16)
        nc.sync.dma_start(slot_token[:], offs)
        for e in (1, 2, 3):
            load_w2(e, 0, N)
        for e in (4, 5):
            load_w2(e, 0, HALF)
        token_slot = []
        gates = []
        for r, pos in enumerate((pos1, pos2)):
            lst = keep.tile([P, T // 16], U16, name=f"token_slot_{r}")
            nc.sync.dma_start(lst[:], pos)
            token_slot.append(lst)
        for r in range(2):
            g = keep.tile([P, T], F32, name=f"gate_{r}")
            nc.sync.dma_start(out=g[:], in_=gate[r])
            gates.append(g)
        for e in (0, 4, 5):
            load_w2(e, HALF, N)

        w1_scale = keep.tile([P, H], U8, align_bytes=64)
        nc.vector.tensor_copy(
            out=w1_scale[:].rearrange("p (t m) -> p t m", t=PACK),
            in_=w1_scale_raw[:].rearrange("p (m t) -> p t m", t=PACK),
        )
        w1_code = keep.tile([P, H], I32, align_bytes=64)
        nc.vector.tensor_copy(
            out=w1_code[:].rearrange("p (t m) -> p t m", t=PACK),
            in_=w1_raw[:].rearrange("p (m t) -> p t m", t=PACK),
        )
        h_pairs = []
        for u in range(2):
            pairs = keep.tile([P, T], U32, name=f"h_pairs_{u}")
            for t0 in range(0, T, TOK):
                bank = psum.tile([P, 2, TOK], F32, tag=f"bank_{3 * u + t0 // TOK}", name="bank1")
                for v in range(2):
                    cols = slice((2 * u + v) * P, (2 * u + v + 1) * P)
                    nc.tensor.matmul_mx(
                        out=bank[:, v, :],
                        lhsT=w1_code[:, cols].bitcast(FP8X4),
                        lhsT_scale=w1_scale[:, cols],
                        rhs=x_code[:, t0 : t0 + TOK].bitcast(FP8X4),
                        rhs_scale=x_scale[:, t0 : t0 + TOK],
                        start=True,
                        stop=True,
                    )
                nc.scalar.activation(
                    out=pairs[:, t0 : t0 + TOK].bitcast(BF16).rearrange("p (n v) -> p n v", v=2),
                    in_=bank[:].rearrange("p v n -> p n v"),
                    func=GELU,
                )
            h_pairs.append(pairs)

        early = ((0,), (1, 2, 3, 4), (5,))
        late = ((1, 2), (3, 0, 4, 5))
        groups = (early, early, ((1, 2), (3,), (0, 4), (5,)), late)
        w2_grouped, w2_code, w2_scale = {}, {}, {}

        def round_w2(b, e, copy, tag=None):
            group = [g for g in groups[b] if e in g][0]
            if (b, group) not in w2_grouped:
                name = f"w2_grouped_{b}_{group[0]}"
                w2_grouped[b, group] = keep.tile(
                    [P, len(group), P * PACK], BF16, align_bytes=64, name=name, tag=tag or name
                )
            dst, src = w2_grouped[b, group][:, group.index(e), :], w2_raw[e, b]
            if copy is on_gpsimd:
                copy(out=dst.rearrange("p (n j) -> p n j", j=PACK), in_=src.rearrange("p j n -> p n j"))
            else:
                copy(
                    out=dst.rearrange("p (c i j) -> p c j i", i=4, j=PACK),
                    in_=src.rearrange("p j (c i) -> p c j i", i=4),
                )

        def on_gpsimd(out, in_):
            nc.gpsimd.tensor_scalar(out, in_, 1.0, 0.0, MULT, ADD)

        def quantise_w2(b, g, tag=None):
            group = groups[b][g]
            name = f"w2_code_{b}_{g}"
            code = keep.tile([P, len(group) * P], U32, align_bytes=64, name=name, tag=tag or name)
            name = f"w2_scale_{b}_{g}"
            scale = keep.tile([P, len(group) * P], U8, align_bytes=64, name=name, tag=name)
            nc.vector.quantize_mx(
                out=code[:].bitcast(FP8X4),
                scales=scale[:],
                in_=w2_grouped[b, group][:].rearrange("p e w -> p (e w)"),
            )
            for k, e in enumerate(group):
                w2_code[b, e] = code[:, k * P : (k + 1) * P]
                w2_scale[b, e] = scale[:, k * P : (k + 1) * P]

        h_code, h_scale, picked, grouped = [], [], {}, {}
        for s in range(S // PIECE):
            h_code.append(keep.tile([P, PIECE], U32, align_bytes=64, name=f"h_code_{s}"))
            h_scale.append(keep.tile([P, PIECE], U8, align_bytes=64, name=f"h_scale_{s}"))

        def gather_h(s, u, tag):
            if u == 0:
                picked[s] = keep.tile([P, 2, PIECE], U32, align_bytes=64, name=f"picked_{s}", tag=tag)
            cols = slice(s * PIECE // 16, (s + 1) * PIECE // 16)
            nc.vector.tensor_copy(out=picked[s][:, u, :], in_=h_pairs[u][:].indirect(slot_token[:, cols]))

        def weave_h(s, copy, word):
            grouped[s] = keep.tile([P, PIECE * PACK], BF16, align_bytes=64, name=f"h_grouped_{s}", tag=f"h_grouped_{s}")
            copy(
                out=grouped[s][:].bitcast(word).rearrange("p (n u) -> p n u", u=2),
                in_=picked[s][:].bitcast(word).rearrange("p u n -> p n u"),
            )

        def quantise_h(s):
            nc.vector.quantize_mx(out=h_code[s][:].bitcast(FP8X4), scales=h_scale[s][:], in_=grouped[s][:])

        y = [keep.tile([P, S], F32, name=f"y_{b}") for b in range(NB)]

        def experts(b):
            for s in range(S // PIECE):
                bank = psum.tile([P, PIECE], F32, tag=f"bank_{3 * (b % 2) + s}", name="bank2")
                for v in range(2):
                    e = 2 * s + v
                    nc.tensor.matmul_mx(
                        out=bank[:, v * C : (v + 1) * C],
                        lhsT=w2_code[b, e].bitcast(FP8X4),
                        lhsT_scale=w2_scale[b, e],
                        rhs=h_code[s][:, v * C : (v + 1) * C].bitcast(FP8X4),
                        rhs_scale=h_scale[s][:, v * C : (v + 1) * C],
                        start=True,
                        stop=True,
                    )
                nc.scalar.copy(out=y[b][:, s * PIECE : (s + 1) * PIECE], in_=bank[:])

        terms = {}

        def fetch(b, r, lo, hi, tag):
            term = keep.tile([P, hi - lo], F32, align_bytes=64, name=f"term_{b}_{r}_{lo}", tag=tag)
            picked_y = y[b][:].indirect(token_slot[r][:, lo // 16 : hi // 16])
            nc.vector.tensor_tensor(term[:], picked_y, gates[r][:, lo:hi], MULT)
            terms[b, r, lo] = term

        def add_and_store(b, lo, hi):
            total = keep.tile([P, hi - lo], F32, name=f"total_{b}_{lo}")
            nc.vector.tensor_tensor(total[:], terms[b, 0, lo][:], terms[b, 1, lo][:], ADD)
            nc.sync.dma_start(out=out[b * P : (b + 1) * P, lo:hi], in_=total[:])

        ident = keep.tile([P, P], F32)
        make_identity(nc, ident[:])
        turned = {}

        def term_columns(b, r, col):
            lo = max(key[2] for key in terms if key[:2] == (b, r) and key[2] <= col)
            return terms[b, r, lo][:, col - lo : col - lo + P]

        def add_turned(b, first, width):
            turned[b] = keep.tile([P, width], F32, name=f"turned_{b}")
            for lo in range(0, width, T // 2):
                bank = psum.tile([P, T // 2], F32, tag=f"bank_{first[lo // (T // 2)]}", name="bank3")
                for c in range(0, T // 2, P):
                    for r in range(2):
                        nc.tensor.matmul(
                            bank[:, c : c + P],
                            term_columns(b, r, lo + c),
                            ident[:],
                            start=(r == 0),
                            stop=(r == 1),
                            is_transpose=True,
                        )
                nc.scalar.copy(out=turned[b][:, lo : lo + T // 2], in_=bank[:])

        def turn_back_and_store(b, first, width):
            total = keep.tile([P, width], F32, name=f"total_{b}")
            for lo in range(0, width, T // 2):
                bank = psum.tile([P, T // 2], F32, tag=f"bank_{first[lo // (T // 2)]}", name="bank4")
                for c in range(0, T // 2, P):
                    nc.tensor.transpose(bank[:, c : c + P], turned[b][:, lo + c : lo + c + P], ident[:])
                nc.scalar.copy(out=total[:, lo : lo + T // 2], in_=bank[:])
                nc.scalar.dma_start(
                    out=out[b * P : (b + 1) * P, lo : lo + T // 2], in_=total[:, lo : lo + T // 2]
                )

        on_vector, on_scalar = nc.vector.tensor_copy, nc.scalar.copy
        for b in range(2):
            round_w2(b, 0, on_vector)
        for b in range(2):
            quantise_w2(b, 0)
        for b, e in ((3, 1), (2, 2), (3, 2), (2, 3)):
            round_w2(b, e, on_gpsimd)
        for b in range(3):
            round_w2(b, 1, on_scalar)
        gather_h(0, 0, "picked_0")
        gather_h(1, 0, "picked_1")
        gather_h(0, 1, None)
        gather_h(1, 1, None)
        gather_h(2, 0, "w2_raw_1_0")
        gather_h(2, 1, None)
        round_w2(0, 2, on_scalar)
        weave_h(0, on_scalar, U32)
        round_w2(1, 2, on_scalar)
        round_w2(0, 3, on_scalar)
        weave_h(1, on_scalar, U32)
        weave_h(2, on_scalar, U32)
        for e in (3, 4):
            round_w2(1, e, on_scalar)
        quantise_h(0)
        round_w2(0, 4, on_vector)
        quantise_h(1)
        quantise_w2(0, 1)
        round_w2(0, 5, on_vector)
        quantise_h(2)
        quantise_w2(0, 2)
        round_w2(1, 5, on_vector, "h_grouped_2")
        quantise_w2(1, 1, "w2_raw_1_0")
        quantise_w2(1, 2)
        experts(0)
        quantise_w2(2, 0, "w2_scale_0_1")
        quantise_w2(3, 0, "w2_code_0_1")
        experts(1)
        quantise_w2(2, 1, "h_grouped_2")
        for e in (0, 4):
            round_w2(2, e, on_scalar, "w2_code_0_2")
        round_w2(2, 5, on_scalar)
        for e in (3, 0, 4, 5):
            round_w2(3, e, on_scalar, "w2_scale_0_2")
        fetch(0, 0, 0, T, "term_a")
        fetch(0, 1, 0, T, "term_b")
        fetch(1, 0, 0, T, "term_c")
        quantise_w2(2, 2)
        quantise_w2(2, 3)
        add_turned(0, (6, 7), T)
        experts(2)
        fetch(1, 1, 0, T, "w2_grouped_2_5")
        quantise_w2(3, 1)
        turn_back_and_store(0, (6, 7), T)
        experts(3)
        for lo in (0, T // 2):
            for r in range(2):
                fetch(2, r, lo, lo + T // 2, f"term_2_{r}_{lo}")
        add_turned(1, (0, 1), T)
        turn_back_and_store(1, (6, 7), T)
        add_turned(2, (3, 1), T)
        turn_back_and_store(2, (4, 5), T)
        cut = 512
        fetch(3, 0, 0, cut, "term_f")
        fetch(3, 1, 0, cut, "term_g")
        fetch(3, 0, cut, T, "term_h")
        add_and_store(3, 0, cut)
        fetch(3, 1, cut, T, "term_i")
        add_and_store(3, cut, T)
